import numpy as np
import ml_dtypes

BF16 = ml_dtypes.bfloat16


def bf(x):
    return np.asarray(x, np.float32).astype(BF16)


def f32(x):
    return np.asarray(x, np.float32)


def f64(x):
    return np.asarray(x).astype(np.float64)


def striped(idx):
    return np.tile(idx.reshape(-1, 16).T, (8, 1))


def rows(idx, k):
    return np.tile(idx, (k, 1))


def look(tab, idx):
    return np.take_along_axis(f64(tab), rows(idx, len(tab)), axis=1)


K, S, V, N, M = 128, 4096, 2048, 2048, 256


def setup_inputs():
    return {"tab": f32(np.random.standard_normal((K, S))), "w": bf(np.random.standard_normal((K, M)) / np.sqrt(K)), "offs": striped(np.random.randint(0, S, N))}


def reference(tab, w, offs):
    idx = offs[:16].T.reshape(-1)
    t = look(tab, idx)
    x = (t >= 0.25) * 0.5
    y = f64(w).T @ x
    return y

@@ -1,0 +1,52 @@
+import concourse.mybir as mybir
+
+BF16, F32, U16 = mybir.dt.bfloat16, mybir.dt.float32, mybir.dt.uint16
+
+P = 128
+S = 4096
+N = 2048
+M = 256
+
+FLOPS = 2 * P * M * N
+
+PIECE = 512
+
+
+def tile_lookup_deq_step_none_kernel(tc, tab, w, offs, out):
+    nc = tc.nc
+    is_ge, mult = mybir.AluOpType.is_ge, mybir.AluOpType.mult
+    with (
+        tc.tile_pool(name="held", bufs=1) as held,
+        tc.tile_pool(name="work", bufs=N // PIECE) as work,
+        tc.psum_pool(name="psum", bufs=N // PIECE) as psum,
+    ):
+        offsets = held.tile([P, N // 16], U16, name="offsets")
+        nc.sync.dma_start(offsets[:], offs)
+
+        table = held.tile([P, S], F32, name="table")
+        nc.sync.dma_start(table[:, : S // 2], tab[:, : S // 2])
+        nc.scalar.dma_start(table[:, S // 2 :], tab[:, S // 2 :])
+        weights = held.tile([P, M], BF16, name="weights")
+        nc.scalar.dma_start(weights[:], w)
+
+        for start in range(0, N, PIECE):
+            columns = slice(start, start + PIECE)
+            piece_offsets = offsets[:, start // 16 : (start + PIECE) // 16]
+
+            step = work.tile([P, PIECE], F32, name="step")
+            nc.vector.tensor_scalar(step[:], table[:].indirect(piece_offsets), 0.25, 0.5, op0=is_ge, op1=mult)
+
+            x = work.tile([P, PIECE], BF16, name="x")
+            nc.scalar.copy(x[:], step[:])
+
+            product_low = psum.tile([P, PIECE], F32, name="product_low")
+            nc.tensor.matmul(product_low[:], weights[:, :P], x[:], start=True, stop=True)
+            product_high = psum.tile([P, PIECE], F32, name="product_high")
+            nc.tensor.matmul(product_high[:], weights[:, P:], x[:], start=True, stop=True)
+
+            out_low = work.tile([P, PIECE], F32, name="out_low")
+            nc.scalar.copy(out_low[:], product_low[:])
+            nc.sync.dma_start(out[:P, columns], out_low[:])
+            out_high = work.tile([P, PIECE], F32, name="out_high")
+            nc.vector.tensor_copy(out_high[:], product_high[:])
+            nc.sync.dma_start(out[P:, columns], out_high[:])

@@ -9,12 +9,15 @@ M = 256
 
 FLOPS = 2 * P * M * N
 
-PIECE = 512
+HALVES = M // P
+PIECE = 256
+LAST = N - PIECE
 
 
 def tile_lookup_deq_step_none_kernel(tc, tab, w, offs, out):
     nc = tc.nc
     is_ge, mult = mybir.AluOpType.is_ge, mybir.AluOpType.mult
+    out_halves = out.rearrange("(h p) n -> p h n", p=P)
     with (
         tc.tile_pool(name="held", bufs=1) as held,
         tc.tile_pool(name="work", bufs=N // PIECE) as work,
@@ -30,23 +33,20 @@ def tile_lookup_deq_step_none_kernel(tc, tab, w, offs, out):
         nc.scalar.dma_start(weights[:], w)
 
         for start in range(0, N, PIECE):
-            columns = slice(start, start + PIECE)
             piece_offsets = offsets[:, start // 16 : (start + PIECE) // 16]
 
             step = work.tile([P, PIECE], F32, name="step")
             nc.vector.tensor_scalar(step[:], table[:].indirect(piece_offsets), 0.25, 0.5, op0=is_ge, op1=mult)
 
-            x = work.tile([P, PIECE], BF16, name="x")
-            nc.scalar.copy(x[:], step[:])
+            x = step[:].bitcast(BF16)[:, 1::2]
 
-            product_low = psum.tile([P, PIECE], F32, name="product_low")
-            nc.tensor.matmul(product_low[:], weights[:, :P], x[:], start=True, stop=True)
-            product_high = psum.tile([P, PIECE], F32, name="product_high")
-            nc.tensor.matmul(product_high[:], weights[:, P:], x[:], start=True, stop=True)
+            product = psum.tile([P, HALVES, PIECE], F32, name="product")
+            for half in range(HALVES):
+                nc.tensor.matmul(product[:, half, :], weights[:, half * P : (half + 1) * P], x, start=True, stop=True)
 
-            out_low = work.tile([P, PIECE], F32, name="out_low")
-            nc.scalar.copy(out_low[:], product_low[:])
-            nc.sync.dma_start(out[:P, columns], out_low[:])
-            out_high = work.tile([P, PIECE], F32, name="out_high")
-            nc.vector.tensor_copy(out_high[:], product_high[:])
-            nc.sync.dma_start(out[P:, columns], out_high[:])
+            result = work.tile([P, HALVES, PIECE], F32, name="result")
+            if start == LAST:
+                nc.vector.tensor_copy(result[:], product[:])
+            else:
+                nc.scalar.copy(result[:], product[:])
+            nc.sync.dma_start(out_halves[:, :, start : start + PIECE], result[:])

@@ -27,10 +27,9 @@ def tile_lookup_deq_step_none_kernel(tc, tab, w, offs, out):
         nc.sync.dma_start(offsets[:], offs)
 
         table = held.tile([P, S], F32, name="table")
-        nc.sync.dma_start(table[:, : S // 2], tab[:, : S // 2])
-        nc.scalar.dma_start(table[:, S // 2 :], tab[:, S // 2 :])
+        nc.sync.dma_start(table[:], tab)
         weights = held.tile([P, M], BF16, name="weights")
-        nc.scalar.dma_start(weights[:], w)
+        nc.sync.dma_start(weights[:], w)
 
         for start in range(0, N, PIECE):
             piece_offsets = offsets[:, start // 16 : (start + PIECE) // 16]

@@ -11,6 +11,7 @@ FLOPS = 2 * P * M * N
 
 HALVES = M // P
 PIECE = 256
+WARM_UPS = 16
 LAST = N - PIECE
 
 
@@ -30,6 +31,12 @@ def tile_lookup_deq_step_none_kernel(tc, tab, w, offs, out):
         nc.sync.dma_start(table[:], tab)
         weights = held.tile([P, M], BF16, name="weights")
         nc.sync.dma_start(weights[:], w)
+
+        zeros = held.tile([P, HALVES * PIECE], BF16, name="zeros")
+        nc.gpsimd.memset(zeros[:], 0.0)
+        warm = psum.tile([P, HALVES * PIECE], F32, name="warm", tag="product")
+        for repeat in range(WARM_UPS):
+            nc.tensor.matmul(warm[:], zeros[:, :P], zeros[:], start=True, stop=True)
 
         for start in range(0, N, PIECE):
             piece_offsets = offsets[:, start // 16 : (start + PIECE) // 16]

import concourse.mybir as mybir

BF16, F32, U16 = mybir.dt.bfloat16, mybir.dt.float32, mybir.dt.uint16

P = 128
S = 4096
N = 2048
M = 256

FLOPS = 2 * P * M * N

HALVES = M // P
PIECE = 256
WARM_UPS = 16
LAST = N - PIECE


def tile_lookup_deq_step_none_kernel(tc, tab, w, offs, out):
    nc = tc.nc
    is_ge, mult = mybir.AluOpType.is_ge, mybir.AluOpType.mult
    out_halves = out.rearrange("(h p) n -> p h n", p=P)
    with (
        tc.tile_pool(name="held", bufs=1) as held,
        tc.tile_pool(name="work", bufs=N // PIECE) as work,
        tc.psum_pool(name="psum", bufs=N // PIECE) as psum,
    ):
        offsets = held.tile([P, N // 16], U16, name="offsets")
        nc.sync.dma_start(offsets[:], offs)

        table = held.tile([P, S], F32, name="table")
        nc.sync.dma_start(table[:], tab)
        weights = held.tile([P, M], BF16, name="weights")
        nc.sync.dma_start(weights[:], w)

        zeros = held.tile([P, HALVES * PIECE], BF16, name="zeros")
        nc.gpsimd.memset(zeros[:], 0.0)
        warm = psum.tile([P, HALVES * PIECE], F32, name="warm", tag="product")
        for repeat in range(WARM_UPS):
            nc.tensor.matmul(warm[:], zeros[:, :P], zeros[:], start=True, stop=True)

        for start in range(0, N, PIECE):
            piece_offsets = offsets[:, start // 16 : (start + PIECE) // 16]

            step = work.tile([P, PIECE], F32, name="step")
            nc.vector.tensor_scalar(step[:], table[:].indirect(piece_offsets), 0.25, 0.5, op0=is_ge, op1=mult)

            x = step[:].bitcast(BF16)[:, 1::2]

            product = psum.tile([P, HALVES, PIECE], F32, name="product")
            for half in range(HALVES):
                nc.tensor.matmul(product[:, half, :], weights[:, half * P : (half + 1) * P], x, start=True, stop=True)

            result = work.tile([P, HALVES, PIECE], F32, name="result")
            if start == LAST:
                nc.vector.tensor_copy(result[:], product[:])
            else:
                nc.scalar.copy(result[:], product[:])
            nc.sync.dma_start(out_halves[:, :, start : start + PIECE], result[:])
